import numpy as np
import ml_dtypes


def mxq(x, axis, fmt="e4m3"):
    dtype, down = {"e4m3": (ml_dtypes.float8_e4m3fn, 7), "e5m2": (ml_dtypes.float8_e5m2, 14)}[fmt]
    v = np.moveaxis(np.asarray(x, np.float32).astype(ml_dtypes.bfloat16).astype(np.float64), axis, -1)
    blocks = v.reshape(v.shape[:-1] + (-1, 32))
    amax = np.abs(blocks).max(-1, keepdims=True)
    byte = np.maximum(np.where(amax > 0, np.frexp(amax)[1] - 1 + 127, 0) - down, 1)
    scale = np.exp2(byte - 127.0)
    codes = (blocks / scale).astype(np.float32).astype(dtype).astype(np.float64)
    return np.moveaxis((codes * scale).reshape(v.shape), -1, axis)


WIDE = False


def mx_kscale(k):
    if not WIDE:
        return np.ones(k)
    levels = np.array([30, -30])
    if k % 512:
        return np.exp2(np.random.permutation(np.resize(levels, k // 32))).repeat(32)
    a = np.empty((k // 512, 16))
    for p in range(k // 512):
        a[p, :8] = np.random.permutation(np.resize(levels, 8))
        for g in range(8):
            far = levels[np.abs(levels - a[p, g]) >= 10]
            a[p, g + 8] = far[np.random.randint(len(far))]
    return np.exp2(a.ravel()).repeat(32)


def f64(x):
    return np.asarray(x).astype(np.float64)


def striped(idx):
    return np.tile(np.asarray(idx).reshape(-1, 16).T, (8, 1)).astype(np.uint16)


def unstriped(offs):
    return offs[:16].T.reshape(-1).astype(np.int64)


E2M1 = np.array([0.0, 0.5, 1.0, 1.5, 2.0, 3.0, 4.0, 6.0, -0.0, -0.5, -1.0, -1.5, -2.0, -3.0, -4.0, -6.0])


def pack_weight(w, fmt):
    k, n = w.shape
    w = f64(np.asarray(w, np.float32).astype(ml_dtypes.bfloat16)).reshape(k // 32, 32, n)
    amax = np.abs(w).max(1)
    if fmt in ("e4m3", "e5m2"):
        byte = np.frexp(amax)[1] - 1 + 127 - (7 if fmt == "e4m3" else 14)
    else:
        mant, ex = np.frexp(amax / 6.0)
        byte = np.where(mant > 0.5, ex, ex - 1) + 127
    byte = np.clip(np.where(amax > 0, byte, 1), 1, 254)
    scaled = (w * np.exp2(127.0 - byte)[:, None, :]).reshape(k, n).astype(np.float32)
    by_word = np.ascontiguousarray(scaled.reshape(k // 512, 128, 4, n).transpose(0, 1, 3, 2))
    if fmt in ("e4m3", "e5m2"):
        words = by_word.astype(ml_dtypes.float8_e4m3fn if fmt == "e4m3" else ml_dtypes.float8_e5m2).view(np.uint8)
    else:
        c = by_word.astype(ml_dtypes.float4_e2m1fn).view(np.uint8) & 0xF
        words = (c[..., 0::2] | (c[..., 1::2] << 4)).reshape(k // 512, 128, 2 * n)
    return np.ascontiguousarray(words), np.ascontiguousarray(byte.astype(np.uint8).reshape(k // 512, 16, n))


def unpack_weight(words, scales, fmt):
    g, _, n = scales.shape
    words = np.ascontiguousarray(words).reshape(g, 128, n, -1)
    if fmt in ("e4m3", "e5m2"):
        vals = words.view(ml_dtypes.float8_e4m3fn if fmt == "e4m3" else ml_dtypes.float8_e5m2).astype(np.float64)
    else:
        nib = np.empty((g, 128, n, 4), np.uint8)
        nib[..., 0::2] = words & 0xF
        nib[..., 1::2] = words >> 4
        vals = E2M1[nib]
    vals = vals * np.repeat(np.exp2(scales.astype(np.float64) - 127.0), 8, axis=1)[..., None]
    return vals.transpose(0, 1, 3, 2).reshape(g * 512, n)


K, T, J, R, O, N, E = 512, 1024, 256, 512, 256, 256, 1024


def setup_inputs():
    n = np.random.standard_normal
    idx = np.random.permutation(T)[:J]
    idx2 = np.random.permutation(J)[:O]
    idx3 = np.random.permutation(O)[:O]
    idx4 = np.random.permutation(T)[:O]
    idx5 = np.random.permutation(E)[:O]
    fk = mx_kscale(K)
    fr = mx_kscale(R)
    xtp = pack_weight(n((K, T)) / fk[:, None], "e4m3")
    wp = pack_weight(n((K, R)) * 1 / np.sqrt(K) * fk[:, None] * fr, "e2m1")
    wbp = pack_weight(n((R, N)) * 1 / np.sqrt(R) / fr[:, None], "e5m2")
    wsp = pack_weight(n((K, N)) * 1 / np.sqrt(K) * fk[:, None], "e5m2")
    return {
        "xt_words": xtp[0],
        "xt_scales": xtp[1],
        "w_words": wp[0],
        "w_scales": wp[1],
        "sa": (np.random.uniform(0.5, 1.6, (R, 1))).astype(np.float32),
        "sb": (np.random.uniform(0.5, 1.6, (R, 1))).astype(np.float32),
        "wb_words": wbp[0],
        "wb_scales": wbp[1],
        "ws_words": wsp[0],
        "ws_scales": wsp[1],
        "offs": striped(idx),
        "offs2": striped(idx2),
        "offs3": striped(idx3),
        "offs4": striped(idx4),
        "offs5": striped(idx5),
    }


def reference(xt_words, xt_scales, w_words, w_scales, sa, sb, wb_words, wb_scales, ws_words, ws_scales, offs, offs2, offs3, offs4, offs5):
    idx = unstriped(offs)
    idx2 = unstriped(offs2)
    idx3 = unstriped(offs3)
    idx4 = unstriped(offs4)
    idx5 = unstriped(offs5)
    xtu = unpack_weight(xt_words, xt_scales, "e4m3")
    wu = unpack_weight(w_words, w_scales, "e2m1")
    wbu = unpack_weight(wb_words, wb_scales, "e5m2")
    wsu = unpack_weight(ws_words, ws_scales, "e5m2")
    xtidxg = xtu[:, idx]
    a = wu.T @ xtidxg
    ca = a[:, idx2] * f64(sa)
    hid = np.abs(ca - ca[:, idx3] * f64(sb))
    hidq = mxq(hid, 0, "e4m3")
    xtidx4g = xtu[:, idx4]
    p = wbu.T @ hidq + wsu.T @ xtidx4g
    y = np.zeros((N, E))
    y[:, idx5] = p
    return y

@@ -1,0 +1,194 @@
+from contextlib import ExitStack
+
+import concourse.mybir as mybir
+
+K, T, J, R, O, N, E = 512, 1024, 256, 512, 256, 256, 1024
+FLOPS = 2 * K * R * J + 2 * R * N * O + 2 * K * N * O
+
+F32 = mybir.dt.float32
+BF16 = mybir.dt.bfloat16
+I32 = mybir.dt.int32
+U32 = mybir.dt.uint32
+U16 = mybir.dt.uint16
+U8 = mybir.dt.uint8
+E4M3 = mybir.dt.float8_e4m3fn_x4
+E5M2 = mybir.dt.float8_e5m2_x4
+E2M1 = mybir.dt.float4_e2m1fn_x4
+ALU = mybir.AluOpType
+ACT = mybir.ActivationFunctionType
+
+P = 128
+PACK = 4
+QUADS = 4
+HALF = 128
+LIST_COLS = HALF // 16
+
+
+def tile_list_chainneighbour_solo_further_scattered_kernel(
+    tc, xt_words, xt_scales, w_words, w_scales, sa, sb, wb_words, wb_scales, ws_words, ws_scales,
+    offs, offs2, offs3, offs4, offs5, out,
+):
+    nc = tc.nc
+    with ExitStack() as ctx:
+        pool = ctx.enter_context(tc.tile_pool(name="held", bufs=1))
+        psum = ctx.enter_context(tc.psum_pool(name="psum", bufs=1))
+
+        def sb_tile(name, shape, dtype):
+            return pool.tile(shape, dtype, name=name, align_bytes=64)
+
+        def load_list(name, src):
+            tile = sb_tile(name, [P, 16], U16)
+            nc.sync.dma_start(tile[:], src)
+            return tile
+
+        def half_of(lst, h):
+            return lst[:, h * LIST_COLS : (h + 1) * LIST_COLS]
+
+        def words_of(dram):
+            return dram[0].rearrange("p n t -> p (n t)").bitcast(I32)
+
+        def load_scale_rows(plane, dram):
+            for q in range(QUADS):
+                nc.sync.dma_start(plane[32 * q : 32 * q + 4, :].bitcast(I32), dram[0, 4 * q : 4 * q + 4, :].bitcast(I32))
+
+        xt_plane = sb_tile("xt_plane", [P, T], U8)
+        w_plane_raw = sb_tile("w_plane_raw", [P, R], U8)
+        ws_plane = sb_tile("ws_plane", [P, N], U8)
+        wb_plane = sb_tile("wb_plane", [P, N], U8)
+        for plane in (xt_plane, w_plane_raw, ws_plane, wb_plane):
+            nc.vector.memset(plane[:].bitcast(I32), 0)
+        pages = [sb_tile("page%d" % m, [P, E], F32) for m in range(2)]
+        for page in pages:
+            nc.vector.memset(page[:], 0.0)
+
+        l1 = load_list("l1", offs)
+        xt_codes = sb_tile("xt_codes", [P, T], U32)
+        nc.sync.dma_start(xt_codes[:].bitcast(I32), words_of(xt_words))
+        load_scale_rows(xt_plane, xt_scales)
+        w_rows = sb_tile("w_rows", [4, QUADS, R // 4], I32)
+        nc.scalar.dma_start(w_rows[:], w_scales[0].bitcast(I32).rearrange("(q r) c -> r q c", r=4))
+        w_raw = sb_tile("w_raw", [P, R], U16)
+        nc.scalar.dma_start(w_raw[:].bitcast(I32), w_words[0].bitcast(I32))
+        sa_t = sb_tile("sa_t", [P, PACK], F32)
+        sb_t = sb_tile("sb_t", [P, PACK], F32)
+        nc.gpsimd.dma_start(sa_t[:], sa.rearrange("(p t) o -> p (t o)", t=PACK))
+        nc.gpsimd.dma_start(sb_t[:], sb.rearrange("(p t) o -> p (t o)", t=PACK))
+        l2 = load_list("l2", offs2)
+        l3 = load_list("l3", offs3)
+        l4 = load_list("l4", offs4)
+        ws_codes = sb_tile("ws_codes", [P, N], U32)
+        wb_codes = sb_tile("wb_codes", [P, N], U32)
+        nc.sync.dma_start(ws_codes[:].bitcast(I32), words_of(ws_words))
+        load_scale_rows(ws_plane, ws_scales)
+        nc.sync.dma_start(wb_codes[:].bitcast(I32), words_of(wb_words))
+        load_scale_rows(wb_plane, wb_scales)
+        l5 = load_list("l5", offs5)
+
+        w_codes = sb_tile("w_codes", [P, PACK, P], U16)
+        nc.scalar.copy(w_codes[:], w_raw[:].rearrange("p (m t) -> p t m", t=PACK))
+        for q in range(QUADS):
+            nc.vector.tensor_copy(w_plane_raw[32 * q : 32 * q + 4, :].bitcast(I32), w_rows[:, q, :])
+        x1_plane = sb_tile("x1_plane", [P, J], U8)
+        nc.vector.tensor_copy(x1_plane[:], xt_plane[:].indirect(l1[:]))
+        w_plane = sb_tile("w_plane", [P, PACK, P], U8)
+        nc.vector.tensor_copy(w_plane[:], w_plane_raw[:].rearrange("p (m t) -> p t m", t=PACK))
+        x1_codes = sb_tile("x1_codes", [P, J], U32)
+        nc.vector.tensor_copy(x1_codes[:], xt_codes[:].indirect(l1[:]))
+
+        a_tiles = []
+        for t in range(PACK):
+            a_ps = psum.tile([P, J], F32, name="a_ps%d" % t)
+            nc.tensor.matmul_mx(
+                out=a_ps[:],
+                lhsT=w_codes[:, t, :].bitcast(E2M1),
+                lhsT_scale=w_plane[:, t, :],
+                rhs=x1_codes[:].bitcast(E4M3),
+                rhs_scale=x1_plane[:],
+                start=True,
+                stop=True,
+            )
+            a_t = sb_tile("a%d" % t, [P, J], F32)
+            nc.vector.tensor_copy(a_t[:], a_ps[:])
+            a_tiles.append(a_t)
+
+        x4_plane = sb_tile("x4_plane", [P, O], U8)
+        x4_codes = sb_tile("x4_codes", [P, O], U32)
+        nc.vector.tensor_copy(x4_plane[:], xt_plane[:].indirect(l4[:]))
+        nc.vector.tensor_copy(x4_codes[:], xt_codes[:].indirect(l4[:]))
+
+        p_ps = {}
+        for h in range(2):
+            cols = slice(h * HALF, (h + 1) * HALF)
+            for m in range(2):
+                rows = slice(m * P, (m + 1) * P)
+                p_ps[h, m] = psum.tile([P, HALF], F32, name="p_ps%d%d" % (h, m))
+                nc.tensor.matmul_mx(
+                    out=p_ps[h, m][:],
+                    lhsT=ws_codes[:, rows].bitcast(E5M2),
+                    lhsT_scale=ws_plane[:, rows],
+                    rhs=x4_codes[:, cols].bitcast(E4M3),
+                    rhs_scale=x4_plane[:, cols],
+                    start=True,
+                    stop=False,
+                )
+
+        ca_tiles = []
+        for t in range(PACK):
+            ca_t = sb_tile("ca%d" % t, [P, O], F32)
+            for h in range(2):
+                nc.scalar.activation(
+                    ca_t[:, h * HALF : (h + 1) * HALF], a_tiles[t][:].indirect(half_of(l2, h)), ACT.Copy,
+                    scale=sa_t[:, t : t + 1],
+                )
+            ca_tiles.append(ca_t)
+
+        diff = []
+        for h in range(2):
+            cols = slice(h * HALF, (h + 1) * HALF)
+            cb = sb_tile("cb%d" % h, [P, PACK, HALF], F32)
+            d = sb_tile("diff%d" % h, [P, PACK, HALF], F32)
+            mag = sb_tile("mag%d" % h, [P, PACK, HALF], F32) if h == 0 else None
+            for t in range(PACK):
+                nc.scalar.activation(
+                    cb[:, t, :], ca_tiles[t][:].indirect(half_of(l3, h)), ACT.Copy, scale=sb_t[:, t : t + 1]
+                )
+                nc.vector.tensor_tensor(d[:, t, :], ca_tiles[t][:, cols], cb[:, t, :], ALU.subtract)
+                if h == 0:
+                    nc.vector.scalar_tensor_tensor(mag[:, t, :], d[:, t, :], -1.0, d[:, t, :], ALU.mult, ALU.max)
+            if h == 0:
+                hid0 = sb_tile("hid0", [P, HALF, PACK], BF16)
+                nc.vector.tensor_copy(
+                    hid0[:].rearrange("p (c i) t -> p c t i", i=4), mag[:].rearrange("p t (c i) -> p c t i", i=4)
+                )
+            diff.append(d)
+        hid1 = sb_tile("hid1", [P, HALF, PACK], BF16)
+        nc.scalar.activation(
+            hid1[:].rearrange("p (c i) t -> p c t i", i=4), diff[1][:].rearrange("p t (c i) -> p c t i", i=4), ACT.Abs
+        )
+
+        for h, hid in enumerate((hid0, hid1)):
+            h_codes = sb_tile("h_codes%d" % h, [P, HALF], U32)
+            h_plane = sb_tile("h_plane%d" % h, [P, HALF], U8)
+            nc.vector.quantize_mx(
+                out=h_codes[:].bitcast(E4M3), scales=h_plane[:], in_=hid[:].rearrange("p o t -> p (o t)")
+            )
+            for m in range(2):
+                rows = slice(m * P, (m + 1) * P)
+                nc.tensor.matmul_mx(
+                    out=p_ps[h, m][:],
+                    lhsT=wb_codes[:, rows].bitcast(E5M2),
+                    lhsT_scale=wb_plane[:, rows],
+                    rhs=h_codes[:].bitcast(E4M3),
+                    rhs_scale=h_plane[:],
+                    start=False,
+                    stop=True,
+                )
+            p0 = sb_tile("p0_%d" % h, [P, HALF], F32)
+            p1 = sb_tile("p1_%d" % h, [P, HALF], F32)
+            nc.vector.tensor_copy(p0[:], p_ps[h, 0][:])
+            nc.scalar.copy(p1[:], p_ps[h, 1][:])
+            nc.vector.tensor_copy(pages[0][:].indirect(half_of(l5, h)), p0[:])
+            nc.scalar.activation(pages[1][:].indirect(half_of(l5, h)), p1[:], ACT.Copy)
+
+        nc.sync.dma_start(out[0:P, :], pages[0][:])
+        nc.scalar.dma_start(out[P : 2 * P, :], pages[1][:])

@@ -22,6 +22,7 @@ PACK = 4
 QUADS = 4
 HALF = 128
 LIST_COLS = HALF // 16
+SPLIT = 128
 
 
 def tile_list_chainneighbour_solo_further_scattered_kernel(
@@ -33,8 +34,8 @@ def tile_list_chainneighbour_solo_further_scattered_kernel(
         pool = ctx.enter_context(tc.tile_pool(name="held", bufs=1))
         psum = ctx.enter_context(tc.psum_pool(name="psum", bufs=1))
 
-        def sb_tile(name, shape, dtype):
-            return pool.tile(shape, dtype, name=name, align_bytes=64)
+        def sb_tile(name, shape, dtype, tag=None):
+            return pool.tile(shape, dtype, name=name, tag=tag or name, align_bytes=64)
 
         def load_list(name, src):
             tile = sb_tile(name, [P, 16], U16)
@@ -49,50 +50,52 @@ def tile_list_chainneighbour_solo_further_scattered_kernel(
 
         def load_scale_rows(plane, dram):
             for q in range(QUADS):
-                nc.sync.dma_start(plane[32 * q : 32 * q + 4, :].bitcast(I32), dram[0, 4 * q : 4 * q + 4, :].bitcast(I32))
+                nc.scalar.dma_start(plane[32 * q : 32 * q + 4, :].bitcast(I32), dram[0, 4 * q : 4 * q + 4, :].bitcast(I32))
 
         xt_plane = sb_tile("xt_plane", [P, T], U8)
         w_plane_raw = sb_tile("w_plane_raw", [P, R], U8)
-        ws_plane = sb_tile("ws_plane", [P, N], U8)
-        wb_plane = sb_tile("wb_plane", [P, N], U8)
-        for plane in (xt_plane, w_plane_raw, ws_plane, wb_plane):
+        out_planes = sb_tile("out_planes", [P, 2, N], U8)
+        ws_plane = out_planes[:, 0, :]
+        wb_plane = out_planes[:, 1, :]
+        for plane in (xt_plane, w_plane_raw, out_planes):
             nc.vector.memset(plane[:].bitcast(I32), 0)
         pages = [sb_tile("page%d" % m, [P, E], F32) for m in range(2)]
         for page in pages:
             nc.vector.memset(page[:], 0.0)
 
         l1 = load_list("l1", offs)
+        w_raw = sb_tile("w_raw", [P, R], U16)
+        nc.scalar.dma_start(w_raw[:].bitcast(I32), w_words[0].bitcast(I32))
+        w_rows = sb_tile("w_rows", [4, QUADS, R // 4], I32)
+        nc.sync.dma_start(w_rows[:], w_scales[0].bitcast(I32).rearrange("(q r) c -> r q c", r=4))
         xt_codes = sb_tile("xt_codes", [P, T], U32)
         nc.sync.dma_start(xt_codes[:].bitcast(I32), words_of(xt_words))
         load_scale_rows(xt_plane, xt_scales)
-        w_rows = sb_tile("w_rows", [4, QUADS, R // 4], I32)
-        nc.scalar.dma_start(w_rows[:], w_scales[0].bitcast(I32).rearrange("(q r) c -> r q c", r=4))
-        w_raw = sb_tile("w_raw", [P, R], U16)
-        nc.scalar.dma_start(w_raw[:].bitcast(I32), w_words[0].bitcast(I32))
+        l2 = load_list("l2", offs2)
         sa_t = sb_tile("sa_t", [P, PACK], F32)
         sb_t = sb_tile("sb_t", [P, PACK], F32)
         nc.gpsimd.dma_start(sa_t[:], sa.rearrange("(p t) o -> p (t o)", t=PACK))
-        nc.gpsimd.dma_start(sb_t[:], sb.rearrange("(p t) o -> p (t o)", t=PACK))
-        l2 = load_list("l2", offs2)
         l3 = load_list("l3", offs3)
+        nc.gpsimd.dma_start(sb_t[:], sb.rearrange("(p t) o -> p (t o)", t=PACK))
         l4 = load_list("l4", offs4)
+        out_rows = sb_tile("out_rows", [4, QUADS, 2, N // 4], I32)
+        for i, dram in enumerate((ws_scales, wb_scales)):
+            nc.sync.dma_start(out_rows[:, :, i, :], dram[0].bitcast(I32).rearrange("(q r) c -> r q c", r=4))
         ws_codes = sb_tile("ws_codes", [P, N], U32)
         wb_codes = sb_tile("wb_codes", [P, N], U32)
         nc.sync.dma_start(ws_codes[:].bitcast(I32), words_of(ws_words))
-        load_scale_rows(ws_plane, ws_scales)
         nc.sync.dma_start(wb_codes[:].bitcast(I32), words_of(wb_words))
-        load_scale_rows(wb_plane, wb_scales)
         l5 = load_list("l5", offs5)
 
         w_codes = sb_tile("w_codes", [P, PACK, P], U16)
         nc.scalar.copy(w_codes[:], w_raw[:].rearrange("p (m t) -> p t m", t=PACK))
         for q in range(QUADS):
             nc.vector.tensor_copy(w_plane_raw[32 * q : 32 * q + 4, :].bitcast(I32), w_rows[:, q, :])
-        x1_plane = sb_tile("x1_plane", [P, J], U8)
+        x1_plane = sb_tile("x1_plane", [P, J], U8, tag="x_plane")
         nc.vector.tensor_copy(x1_plane[:], xt_plane[:].indirect(l1[:]))
         w_plane = sb_tile("w_plane", [P, PACK, P], U8)
         nc.vector.tensor_copy(w_plane[:], w_plane_raw[:].rearrange("p (m t) -> p t m", t=PACK))
-        x1_codes = sb_tile("x1_codes", [P, J], U32)
+        x1_codes = sb_tile("x1_codes", [P, J], U32, tag="x_codes")
         nc.vector.tensor_copy(x1_codes[:], xt_codes[:].indirect(l1[:]))
 
         a_tiles = []
@@ -107,14 +110,17 @@ def tile_list_chainneighbour_solo_further_scattered_kernel(
                 start=True,
                 stop=True,
             )
-            a_t = sb_tile("a%d" % t, [P, J], F32)
-            nc.vector.tensor_copy(a_t[:], a_ps[:])
+            a_t = sb_tile("a%d" % t, [P, 2 * J], F32)
+            nc.vector.tensor_copy(a_t[:, 0:J], a_ps[:])
             a_tiles.append(a_t)
 
         x4_plane = sb_tile("x4_plane", [P, O], U8)
-        x4_codes = sb_tile("x4_codes", [P, O], U32)
+        x4_codes = sb_tile("x4_codes", [P, O], U32, tag="x_codes")
         nc.vector.tensor_copy(x4_plane[:], xt_plane[:].indirect(l4[:]))
         nc.vector.tensor_copy(x4_codes[:], xt_codes[:].indirect(l4[:]))
+
+        for q in range(QUADS):
+            nc.vector.tensor_copy(out_planes[32 * q : 32 * q + 4, :, :].bitcast(I32), out_rows[:, q, :, :])
 
         p_ps = {}
         for h in range(2):
@@ -135,38 +141,20 @@ def tile_list_chainneighbour_solo_further_scattered_kernel(
         ca_tiles = []
         for t in range(PACK):
             ca_t = sb_tile("ca%d" % t, [P, O], F32)
-            for h in range(2):
-                nc.scalar.activation(
-                    ca_t[:, h * HALF : (h + 1) * HALF], a_tiles[t][:].indirect(half_of(l2, h)), ACT.Copy,
-                    scale=sa_t[:, t : t + 1],
-                )
+            nc.scalar.activation(ca_t[:], a_tiles[t][:].indirect(l2[:]), ACT.Copy, scale=sa_t[:, t : t + 1])
             ca_tiles.append(ca_t)
 
-        diff = []
-        for h in range(2):
+        diff = sb_tile("diff", [P, PACK, HALF], F32)
+
+        def differences(h, cb, planes):
             cols = slice(h * HALF, (h + 1) * HALF)
-            cb = sb_tile("cb%d" % h, [P, PACK, HALF], F32)
-            d = sb_tile("diff%d" % h, [P, PACK, HALF], F32)
-            mag = sb_tile("mag%d" % h, [P, PACK, HALF], F32) if h == 0 else None
-            for t in range(PACK):
+            for t in planes:
                 nc.scalar.activation(
                     cb[:, t, :], ca_tiles[t][:].indirect(half_of(l3, h)), ACT.Copy, scale=sb_t[:, t : t + 1]
                 )
-                nc.vector.tensor_tensor(d[:, t, :], ca_tiles[t][:, cols], cb[:, t, :], ALU.subtract)
-                if h == 0:
-                    nc.vector.scalar_tensor_tensor(mag[:, t, :], d[:, t, :], -1.0, d[:, t, :], ALU.mult, ALU.max)
-            if h == 0:
-                hid0 = sb_tile("hid0", [P, HALF, PACK], BF16)
-                nc.vector.tensor_copy(
-                    hid0[:].rearrange("p (c i) t -> p c t i", i=4), mag[:].rearrange("p t (c i) -> p c t i", i=4)
-                )
-            diff.append(d)
-        hid1 = sb_tile("hid1", [P, HALF, PACK], BF16)
-        nc.scalar.activation(
-            hid1[:].rearrange("p (c i) t -> p c t i", i=4), diff[1][:].rearrange("p t (c i) -> p c t i", i=4), ACT.Abs
-        )
+                nc.vector.tensor_tensor(diff[:, t, :], ca_tiles[t][:, cols], cb[:, t, :], ALU.subtract)
 
-        for h, hid in enumerate((hid0, hid1)):
+        def second_product(h, hid):
             h_codes = sb_tile("h_codes%d" % h, [P, HALF], U32)
             h_plane = sb_tile("h_plane%d" % h, [P, HALF], U8)
             nc.vector.quantize_mx(
@@ -183,12 +171,36 @@ def tile_list_chainneighbour_solo_further_scattered_kernel(
                     start=False,
                     stop=True,
                 )
+
+        def place(h, copy0):
             p0 = sb_tile("p0_%d" % h, [P, HALF], F32)
             p1 = sb_tile("p1_%d" % h, [P, HALF], F32)
-            nc.vector.tensor_copy(p0[:], p_ps[h, 0][:])
+            copy0(p0[:], p_ps[h, 0][:])
             nc.scalar.copy(p1[:], p_ps[h, 1][:])
             nc.vector.tensor_copy(pages[0][:].indirect(half_of(l5, h)), p0[:])
             nc.scalar.activation(pages[1][:].indirect(half_of(l5, h)), p1[:], ACT.Copy)
+            return p0
+
+        cb0 = sb_tile("cb0", [P, PACK, HALF], F32, tag="a2")
+        mag = sb_tile("mag", [P, PACK, HALF], F32)
+        for t in (0, 2):
+            differences(0, cb0, (t, t + 1))
+            pair = diff[:, t : t + 2, :]
+            nc.vector.scalar_tensor_tensor(mag[:, t : t + 2, :], pair, -1.0, pair, ALU.mult, ALU.max)
+        hid0 = sb_tile("hid0", [P, HALF, PACK], BF16)
+        nc.vector.tensor_copy(
+            hid0[:].rearrange("p (c i) t -> p c t i", i=4), mag[:].rearrange("p t (c i) -> p c t i", i=4)
+        )
+        cb1 = sb_tile("cb1", [P, PACK, HALF], F32, tag="a3")
+        differences(1, cb1, range(PACK))
+        second_product(0, hid0)
+        hid1 = sb_tile("hid1", [P, HALF, PACK], BF16)
+        nc.scalar.activation(
+            hid1[:].rearrange("p (c i) t -> p c t i", i=4), diff[:].rearrange("p t (c i) -> p c t i", i=4), ACT.Abs
+        )
+        second_product(1, hid1)
+        pa = place(0, nc.scalar.copy)
+        pb = place(1, nc.vector.tensor_copy)
 
         nc.sync.dma_start(out[0:P, :], pages[0][:])
         nc.scalar.dma_start(out[P : 2 * P, :], pages[1][:])

@@ -20,9 +20,12 @@ ACT = mybir.ActivationFunctionType
 P = 128
 PACK = 4
 QUADS = 4
-HALF = 128
-LIST_COLS = HALF // 16
-SPLIT = 128
+QUAD = 32
+SCALE_ROWS = 4
+WORD_BYTES = 4
+LIST_GROUP = 16
+HALF = O // 2
+RUN = 4
 
 
 def tile_list_chainneighbour_solo_further_scattered_kernel(
@@ -34,69 +37,72 @@ def tile_list_chainneighbour_solo_further_scattered_kernel(
         pool = ctx.enter_context(tc.tile_pool(name="held", bufs=1))
         psum = ctx.enter_context(tc.psum_pool(name="psum", bufs=1))
 
-        def sb_tile(name, shape, dtype, tag=None):
+        def sbuf(name, shape, dtype, tag=None):
             return pool.tile(shape, dtype, name=name, tag=tag or name, align_bytes=64)
 
-        def load_list(name, src):
-            tile = sb_tile(name, [P, 16], U16)
-            nc.sync.dma_start(tile[:], src)
+        def load_list(name, dram):
+            tile = sbuf(name, [P, O // LIST_GROUP], U16)
+            nc.sync.dma_start(tile[:], dram)
             return tile
 
-        def half_of(lst, h):
-            return lst[:, h * LIST_COLS : (h + 1) * LIST_COLS]
+        def half_of(entries, h):
+            width = HALF // LIST_GROUP
+            return entries[:, h * width : (h + 1) * width]
 
         def words_of(dram):
             return dram[0].rearrange("p n t -> p (n t)").bitcast(I32)
 
+        def live_rows(q):
+            return slice(QUAD * q, QUAD * q + SCALE_ROWS)
+
         def load_scale_rows(plane, dram):
             for q in range(QUADS):
-                nc.scalar.dma_start(plane[32 * q : 32 * q + 4, :].bitcast(I32), dram[0, 4 * q : 4 * q + 4, :].bitcast(I32))
+                rows = dram[0, SCALE_ROWS * q : SCALE_ROWS * (q + 1), :]
+                nc.sync.dma_start(plane[live_rows(q), :].bitcast(I32), rows.bitcast(I32))
 
-        xt_plane = sb_tile("xt_plane", [P, T], U8)
-        w_plane_raw = sb_tile("w_plane_raw", [P, R], U8)
-        out_planes = sb_tile("out_planes", [P, 2, N], U8)
-        ws_plane = out_planes[:, 0, :]
-        wb_plane = out_planes[:, 1, :]
-        for plane in (xt_plane, w_plane_raw, out_planes):
+        xt_plane = sbuf("xt_plane", [P, T], U8)
+        w_plane_raw = sbuf("w_plane_raw", [P, R], U8)
+        ws_plane = sbuf("ws_plane", [P, N], U8)
+        wb_plane = sbuf("wb_plane", [P, N], U8)
+        for plane in (xt_plane, w_plane_raw, ws_plane, wb_plane):
             nc.vector.memset(plane[:].bitcast(I32), 0)
-        pages = [sb_tile("page%d" % m, [P, E], F32) for m in range(2)]
+        pages = [sbuf("page%d" % m, [P, E], F32) for m in range(N // P)]
         for page in pages:
             nc.vector.memset(page[:], 0.0)
 
-        l1 = load_list("l1", offs)
-        w_raw = sb_tile("w_raw", [P, R], U16)
-        nc.scalar.dma_start(w_raw[:].bitcast(I32), w_words[0].bitcast(I32))
-        w_rows = sb_tile("w_rows", [4, QUADS, R // 4], I32)
-        nc.sync.dma_start(w_rows[:], w_scales[0].bitcast(I32).rearrange("(q r) c -> r q c", r=4))
-        xt_codes = sb_tile("xt_codes", [P, T], U32)
+        list1 = load_list("l1", offs)
+        xt_codes = sbuf("xt_codes", [P, T], U32)
         nc.sync.dma_start(xt_codes[:].bitcast(I32), words_of(xt_words))
         load_scale_rows(xt_plane, xt_scales)
-        l2 = load_list("l2", offs2)
-        sa_t = sb_tile("sa_t", [P, PACK], F32)
-        sb_t = sb_tile("sb_t", [P, PACK], F32)
+        w_rows = sbuf("w_rows", [SCALE_ROWS, QUADS, R // WORD_BYTES], I32)
+        nc.scalar.dma_start(w_rows[:], w_scales[0].bitcast(I32).rearrange("(q r) c -> r q c", r=SCALE_ROWS))
+        w_raw = sbuf("w_raw", [P, R], U16)
+        nc.scalar.dma_start(w_raw[:].bitcast(I32), w_words[0].bitcast(I32))
+        list2 = load_list("l2", offs2)
+        sa_t = sbuf("sa_t", [P, PACK], F32)
+        sb_t = sbuf("sb_t", [P, PACK], F32)
         nc.gpsimd.dma_start(sa_t[:], sa.rearrange("(p t) o -> p (t o)", t=PACK))
-        l3 = load_list("l3", offs3)
+        list3 = load_list("l3", offs3)
         nc.gpsimd.dma_start(sb_t[:], sb.rearrange("(p t) o -> p (t o)", t=PACK))
-        l4 = load_list("l4", offs4)
-        out_rows = sb_tile("out_rows", [4, QUADS, 2, N // 4], I32)
-        for i, dram in enumerate((ws_scales, wb_scales)):
-            nc.sync.dma_start(out_rows[:, :, i, :], dram[0].bitcast(I32).rearrange("(q r) c -> r q c", r=4))
-        ws_codes = sb_tile("ws_codes", [P, N], U32)
-        wb_codes = sb_tile("wb_codes", [P, N], U32)
+        list4 = load_list("l4", offs4)
+        list5 = load_list("l5", offs5)
+        ws_codes = sbuf("ws_codes", [P, N], U32)
+        wb_codes = sbuf("wb_codes", [P, N], U32)
         nc.sync.dma_start(ws_codes[:].bitcast(I32), words_of(ws_words))
+        load_scale_rows(ws_plane, ws_scales)
         nc.sync.dma_start(wb_codes[:].bitcast(I32), words_of(wb_words))
-        l5 = load_list("l5", offs5)
+        load_scale_rows(wb_plane, wb_scales)
 
-        w_codes = sb_tile("w_codes", [P, PACK, P], U16)
+        w_codes = sbuf("w_codes", [P, PACK, P], U16)
         nc.scalar.copy(w_codes[:], w_raw[:].rearrange("p (m t) -> p t m", t=PACK))
         for q in range(QUADS):
-            nc.vector.tensor_copy(w_plane_raw[32 * q : 32 * q + 4, :].bitcast(I32), w_rows[:, q, :])
-        x1_plane = sb_tile("x1_plane", [P, J], U8, tag="x_plane")
-        nc.vector.tensor_copy(x1_plane[:], xt_plane[:].indirect(l1[:]))
-        w_plane = sb_tile("w_plane", [P, PACK, P], U8)
+            nc.vector.tensor_copy(w_plane_raw[live_rows(q), :].bitcast(I32), w_rows[:, q, :])
+        x1_plane = sbuf("x1_plane", [P, J], U8)
+        nc.vector.tensor_copy(x1_plane[:], xt_plane[:].indirect(list1[:]))
+        w_plane = sbuf("w_plane", [P, PACK, P], U8)
         nc.vector.tensor_copy(w_plane[:], w_plane_raw[:].rearrange("p (m t) -> p t m", t=PACK))
-        x1_codes = sb_tile("x1_codes", [P, J], U32, tag="x_codes")
-        nc.vector.tensor_copy(x1_codes[:], xt_codes[:].indirect(l1[:]))
+        x1_codes = sbuf("x1_codes", [P, J], U32, tag="x_codes")
+        nc.vector.tensor_copy(x1_codes[:], xt_codes[:].indirect(list1[:]))
 
         a_tiles = []
         for t in range(PACK):
@@ -110,22 +116,19 @@ def tile_list_chainneighbour_solo_further_scattered_kernel(
                 start=True,
                 stop=True,
             )
-            a_t = sb_tile("a%d" % t, [P, 2 * J], F32)
+            a_t = sbuf("a%d" % t, [P, 2 * J], F32)
             nc.vector.tensor_copy(a_t[:, 0:J], a_ps[:])
             a_tiles.append(a_t)
 
-        x4_plane = sb_tile("x4_plane", [P, O], U8)
-        x4_codes = sb_tile("x4_codes", [P, O], U32, tag="x_codes")
-        nc.vector.tensor_copy(x4_plane[:], xt_plane[:].indirect(l4[:]))
-        nc.vector.tensor_copy(x4_codes[:], xt_codes[:].indirect(l4[:]))
-
-        for q in range(QUADS):
-            nc.vector.tensor_copy(out_planes[32 * q : 32 * q + 4, :, :].bitcast(I32), out_rows[:, q, :, :])
+        x4_plane = sbuf("x4_plane", [P, O], U8)
+        x4_codes = sbuf("x4_codes", [P, O], U32, tag="x_codes")
+        nc.vector.tensor_copy(x4_plane[:], xt_plane[:].indirect(list4[:]))
+        nc.vector.tensor_copy(x4_codes[:], xt_codes[:].indirect(list4[:]))
 
         p_ps = {}
         for h in range(2):
             cols = slice(h * HALF, (h + 1) * HALF)
-            for m in range(2):
+            for m in range(N // P):
                 rows = slice(m * P, (m + 1) * P)
                 p_ps[h, m] = psum.tile([P, HALF], F32, name="p_ps%d%d" % (h, m))
                 nc.tensor.matmul_mx(
@@ -140,27 +143,33 @@ def tile_list_chainneighbour_solo_further_scattered_kernel(
 
         ca_tiles = []
         for t in range(PACK):
-            ca_t = sb_tile("ca%d" % t, [P, O], F32)
-            nc.scalar.activation(ca_t[:], a_tiles[t][:].indirect(l2[:]), ACT.Copy, scale=sa_t[:, t : t + 1])
+            ca_t = sbuf("ca%d" % t, [P, O], F32)
+            nc.scalar.activation(ca_t[:], a_tiles[t][:].indirect(list2[:]), ACT.Copy, scale=sa_t[:, t : t + 1])
             ca_tiles.append(ca_t)
 
-        diff = sb_tile("diff", [P, PACK, HALF], F32)
+        diff = sbuf("diff", [P, PACK, HALF], F32)
 
-        def differences(h, cb, planes):
+        def differences(h, cb, slices):
             cols = slice(h * HALF, (h + 1) * HALF)
-            for t in planes:
+            for t in slices:
                 nc.scalar.activation(
-                    cb[:, t, :], ca_tiles[t][:].indirect(half_of(l3, h)), ACT.Copy, scale=sb_t[:, t : t + 1]
+                    cb[:, t, :], ca_tiles[t][:].indirect(half_of(list3, h)), ACT.Copy, scale=sb_t[:, t : t + 1]
                 )
                 nc.vector.tensor_tensor(diff[:, t, :], ca_tiles[t][:, cols], cb[:, t, :], ALU.subtract)
 
+        def as_runs(hid, slices):
+            return (
+                hid[:].rearrange("p (c i) t -> p c t i", i=RUN),
+                slices[:].rearrange("p t (c i) -> p c t i", i=RUN),
+            )
+
         def second_product(h, hid):
-            h_codes = sb_tile("h_codes%d" % h, [P, HALF], U32)
-            h_plane = sb_tile("h_plane%d" % h, [P, HALF], U8)
+            h_codes = sbuf("h_codes%d" % h, [P, HALF], U32)
+            h_plane = sbuf("h_plane%d" % h, [P, HALF], U8)
             nc.vector.quantize_mx(
                 out=h_codes[:].bitcast(E4M3), scales=h_plane[:], in_=hid[:].rearrange("p o t -> p (o t)")
             )
-            for m in range(2):
+            for m in range(N // P):
                 rows = slice(m * P, (m + 1) * P)
                 nc.tensor.matmul_mx(
                     out=p_ps[h, m][:],
@@ -172,35 +181,31 @@ def tile_list_chainneighbour_solo_further_scattered_kernel(
                     stop=True,
                 )
 
-        def place(h, copy0):
-            p0 = sb_tile("p0_%d" % h, [P, HALF], F32)
-            p1 = sb_tile("p1_%d" % h, [P, HALF], F32)
-            copy0(p0[:], p_ps[h, 0][:])
+        def place(h, copy_for_page0):
+            p0 = sbuf("p0_%d" % h, [P, HALF], F32)
+            p1 = sbuf("p1_%d" % h, [P, HALF], F32)
+            copy_for_page0(p0[:], p_ps[h, 0][:])
             nc.scalar.copy(p1[:], p_ps[h, 1][:])
-            nc.vector.tensor_copy(pages[0][:].indirect(half_of(l5, h)), p0[:])
-            nc.scalar.activation(pages[1][:].indirect(half_of(l5, h)), p1[:], ACT.Copy)
-            return p0
+            nc.vector.tensor_copy(pages[0][:].indirect(half_of(list5, h)), p0[:])
+            nc.scalar.activation(pages[1][:].indirect(half_of(list5, h)), p1[:], ACT.Copy)
 
-        cb0 = sb_tile("cb0", [P, PACK, HALF], F32, tag="a2")
-        mag = sb_tile("mag", [P, PACK, HALF], F32)
-        for t in (0, 2):
+        cb0 = sbuf("cb0", [P, PACK, HALF], F32, tag="a2")
+        mag = sbuf("mag", [P, PACK, HALF], F32)
+        for t in range(0, PACK, 2):
             differences(0, cb0, (t, t + 1))
             pair = diff[:, t : t + 2, :]
             nc.vector.scalar_tensor_tensor(mag[:, t : t + 2, :], pair, -1.0, pair, ALU.mult, ALU.max)
-        hid0 = sb_tile("hid0", [P, HALF, PACK], BF16)
-        nc.vector.tensor_copy(
-            hid0[:].rearrange("p (c i) t -> p c t i", i=4), mag[:].rearrange("p t (c i) -> p c t i", i=4)
-        )
-        cb1 = sb_tile("cb1", [P, PACK, HALF], F32, tag="a3")
+        hid0 = sbuf("hid0", [P, HALF, PACK], BF16)
+        nc.vector.tensor_copy(*as_runs(hid0, mag))
+
+        cb1 = sbuf("cb1", [P, PACK, HALF], F32, tag="a3")
         differences(1, cb1, range(PACK))
         second_product(0, hid0)
-        hid1 = sb_tile("hid1", [P, HALF, PACK], BF16)
-        nc.scalar.activation(
-            hid1[:].rearrange("p (c i) t -> p c t i", i=4), diff[:].rearrange("p t (c i) -> p c t i", i=4), ACT.Abs
-        )
+        hid1 = sbuf("hid1", [P, HALF, PACK], BF16)
+        nc.scalar.activation(*as_runs(hid1, diff), ACT.Abs)
         second_product(1, hid1)
-        pa = place(0, nc.scalar.copy)
-        pb = place(1, nc.vector.tensor_copy)
+        place(0, nc.scalar.copy)
+        place(1, nc.vector.tensor_copy)
 
         nc.sync.dma_start(out[0:P, :], pages[0][:])
         nc.scalar.dma_start(out[P : 2 * P, :], pages[1][:])

from contextlib import ExitStack

import concourse.mybir as mybir

K, T, J, R, O, N, E = 512, 1024, 256, 512, 256, 256, 1024
FLOPS = 2 * K * R * J + 2 * R * N * O + 2 * K * N * O

F32 = mybir.dt.float32
BF16 = mybir.dt.bfloat16
I32 = mybir.dt.int32
U32 = mybir.dt.uint32
U16 = mybir.dt.uint16
U8 = mybir.dt.uint8
E4M3 = mybir.dt.float8_e4m3fn_x4
E5M2 = mybir.dt.float8_e5m2_x4
E2M1 = mybir.dt.float4_e2m1fn_x4
ALU = mybir.AluOpType
ACT = mybir.ActivationFunctionType

P = 128
PACK = 4
QUADS = 4
QUAD = 32
SCALE_ROWS = 4
WORD_BYTES = 4
LIST_GROUP = 16
HALF = O // 2
RUN = 4


def tile_list_chainneighbour_solo_further_scattered_kernel(
    tc, xt_words, xt_scales, w_words, w_scales, sa, sb, wb_words, wb_scales, ws_words, ws_scales,
    offs, offs2, offs3, offs4, offs5, out,
):
    nc = tc.nc
    with ExitStack() as ctx:
        pool = ctx.enter_context(tc.tile_pool(name="held", bufs=1))
        psum = ctx.enter_context(tc.psum_pool(name="psum", bufs=1))

        def sbuf(name, shape, dtype, tag=None):
            return pool.tile(shape, dtype, name=name, tag=tag or name, align_bytes=64)

        def load_list(name, dram):
            tile = sbuf(name, [P, O // LIST_GROUP], U16)
            nc.sync.dma_start(tile[:], dram)
            return tile

        def half_of(entries, h):
            width = HALF // LIST_GROUP
            return entries[:, h * width : (h + 1) * width]

        def words_of(dram):
            return dram[0].rearrange("p n t -> p (n t)").bitcast(I32)

        def live_rows(q):
            return slice(QUAD * q, QUAD * q + SCALE_ROWS)

        def load_scale_rows(plane, dram):
            for q in range(QUADS):
                rows = dram[0, SCALE_ROWS * q : SCALE_ROWS * (q + 1), :]
                nc.sync.dma_start(plane[live_rows(q), :].bitcast(I32), rows.bitcast(I32))

        xt_plane = sbuf("xt_plane", [P, T], U8)
        w_plane_raw = sbuf("w_plane_raw", [P, R], U8)
        ws_plane = sbuf("ws_plane", [P, N], U8)
        wb_plane = sbuf("wb_plane", [P, N], U8)
        for plane in (xt_plane, w_plane_raw, ws_plane, wb_plane):
            nc.vector.memset(plane[:].bitcast(I32), 0)
        pages = [sbuf("page%d" % m, [P, E], F32) for m in range(N // P)]
        for page in pages:
            nc.vector.memset(page[:], 0.0)

        list1 = load_list("l1", offs)
        xt_codes = sbuf("xt_codes", [P, T], U32)
        nc.sync.dma_start(xt_codes[:].bitcast(I32), words_of(xt_words))
        load_scale_rows(xt_plane, xt_scales)
        w_rows = sbuf("w_rows", [SCALE_ROWS, QUADS, R // WORD_BYTES], I32)
        nc.scalar.dma_start(w_rows[:], w_scales[0].bitcast(I32).rearrange("(q r) c -> r q c", r=SCALE_ROWS))
        w_raw = sbuf("w_raw", [P, R], U16)
        nc.scalar.dma_start(w_raw[:].bitcast(I32), w_words[0].bitcast(I32))
        list2 = load_list("l2", offs2)
        sa_t = sbuf("sa_t", [P, PACK], F32)
        sb_t = sbuf("sb_t", [P, PACK], F32)
        nc.gpsimd.dma_start(sa_t[:], sa.rearrange("(p t) o -> p (t o)", t=PACK))
        list3 = load_list("l3", offs3)
        nc.gpsimd.dma_start(sb_t[:], sb.rearrange("(p t) o -> p (t o)", t=PACK))
        list4 = load_list("l4", offs4)
        list5 = load_list("l5", offs5)
        ws_codes = sbuf("ws_codes", [P, N], U32)
        wb_codes = sbuf("wb_codes", [P, N], U32)
        nc.sync.dma_start(ws_codes[:].bitcast(I32), words_of(ws_words))
        load_scale_rows(ws_plane, ws_scales)
        nc.sync.dma_start(wb_codes[:].bitcast(I32), words_of(wb_words))
        load_scale_rows(wb_plane, wb_scales)

        w_codes = sbuf("w_codes", [P, PACK, P], U16)
        nc.scalar.copy(w_codes[:], w_raw[:].rearrange("p (m t) -> p t m", t=PACK))
        for q in range(QUADS):
            nc.vector.tensor_copy(w_plane_raw[live_rows(q), :].bitcast(I32), w_rows[:, q, :])
        x1_plane = sbuf("x1_plane", [P, J], U8)
        nc.vector.tensor_copy(x1_plane[:], xt_plane[:].indirect(list1[:]))
        w_plane = sbuf("w_plane", [P, PACK, P], U8)
        nc.vector.tensor_copy(w_plane[:], w_plane_raw[:].rearrange("p (m t) -> p t m", t=PACK))
        x1_codes = sbuf("x1_codes", [P, J], U32, tag="x_codes")
        nc.vector.tensor_copy(x1_codes[:], xt_codes[:].indirect(list1[:]))

        a_tiles = []
        for t in range(PACK):
            a_ps = psum.tile([P, J], F32, name="a_ps%d" % t)
            nc.tensor.matmul_mx(
                out=a_ps[:],
                lhsT=w_codes[:, t, :].bitcast(E2M1),
                lhsT_scale=w_plane[:, t, :],
                rhs=x1_codes[:].bitcast(E4M3),
                rhs_scale=x1_plane[:],
                start=True,
                stop=True,
            )
            a_t = sbuf("a%d" % t, [P, 2 * J], F32)
            nc.vector.tensor_copy(a_t[:, 0:J], a_ps[:])
            a_tiles.append(a_t)

        x4_plane = sbuf("x4_plane", [P, O], U8)
        x4_codes = sbuf("x4_codes", [P, O], U32, tag="x_codes")
        nc.vector.tensor_copy(x4_plane[:], xt_plane[:].indirect(list4[:]))
        nc.vector.tensor_copy(x4_codes[:], xt_codes[:].indirect(list4[:]))

        p_ps = {}
        for h in range(2):
            cols = slice(h * HALF, (h + 1) * HALF)
            for m in range(N // P):
                rows = slice(m * P, (m + 1) * P)
                p_ps[h, m] = psum.tile([P, HALF], F32, name="p_ps%d%d" % (h, m))
                nc.tensor.matmul_mx(
                    out=p_ps[h, m][:],
                    lhsT=ws_codes[:, rows].bitcast(E5M2),
                    lhsT_scale=ws_plane[:, rows],
                    rhs=x4_codes[:, cols].bitcast(E4M3),
                    rhs_scale=x4_plane[:, cols],
                    start=True,
                    stop=False,
                )

        ca_tiles = []
        for t in range(PACK):
            ca_t = sbuf("ca%d" % t, [P, O], F32)
            nc.scalar.activation(ca_t[:], a_tiles[t][:].indirect(list2[:]), ACT.Copy, scale=sa_t[:, t : t + 1])
            ca_tiles.append(ca_t)

        diff = sbuf("diff", [P, PACK, HALF], F32)

        def differences(h, cb, slices):
            cols = slice(h * HALF, (h + 1) * HALF)
            for t in slices:
                nc.scalar.activation(
                    cb[:, t, :], ca_tiles[t][:].indirect(half_of(list3, h)), ACT.Copy, scale=sb_t[:, t : t + 1]
                )
                nc.vector.tensor_tensor(diff[:, t, :], ca_tiles[t][:, cols], cb[:, t, :], ALU.subtract)

        def as_runs(hid, slices):
            return (
                hid[:].rearrange("p (c i) t -> p c t i", i=RUN),
                slices[:].rearrange("p t (c i) -> p c t i", i=RUN),
            )

        def second_product(h, hid):
            h_codes = sbuf("h_codes%d" % h, [P, HALF], U32)
            h_plane = sbuf("h_plane%d" % h, [P, HALF], U8)
            nc.vector.quantize_mx(
                out=h_codes[:].bitcast(E4M3), scales=h_plane[:], in_=hid[:].rearrange("p o t -> p (o t)")
            )
            for m in range(N // P):
                rows = slice(m * P, (m + 1) * P)
                nc.tensor.matmul_mx(
                    out=p_ps[h, m][:],
                    lhsT=wb_codes[:, rows].bitcast(E5M2),
                    lhsT_scale=wb_plane[:, rows],
                    rhs=h_codes[:].bitcast(E4M3),
                    rhs_scale=h_plane[:],
                    start=False,
                    stop=True,
                )

        def place(h, copy_for_page0):
            p0 = sbuf("p0_%d" % h, [P, HALF], F32)
            p1 = sbuf("p1_%d" % h, [P, HALF], F32)
            copy_for_page0(p0[:], p_ps[h, 0][:])
            nc.scalar.copy(p1[:], p_ps[h, 1][:])
            nc.vector.tensor_copy(pages[0][:].indirect(half_of(list5, h)), p0[:])
            nc.scalar.activation(pages[1][:].indirect(half_of(list5, h)), p1[:], ACT.Copy)

        cb0 = sbuf("cb0", [P, PACK, HALF], F32, tag="a2")
        mag = sbuf("mag", [P, PACK, HALF], F32)
        for t in range(0, PACK, 2):
            differences(0, cb0, (t, t + 1))
            pair = diff[:, t : t + 2, :]
            nc.vector.scalar_tensor_tensor(mag[:, t : t + 2, :], pair, -1.0, pair, ALU.mult, ALU.max)
        hid0 = sbuf("hid0", [P, HALF, PACK], BF16)
        nc.vector.tensor_copy(*as_runs(hid0, mag))

        cb1 = sbuf("cb1", [P, PACK, HALF], F32, tag="a3")
        differences(1, cb1, range(PACK))
        second_product(0, hid0)
        hid1 = sbuf("hid1", [P, HALF, PACK], BF16)
        nc.scalar.activation(*as_runs(hid1, diff), ACT.Abs)
        second_product(1, hid1)
        place(0, nc.scalar.copy)
        place(1, nc.vector.tensor_copy)

        nc.sync.dma_start(out[0:P, :], pages[0][:])
        nc.scalar.dma_start(out[P : 2 * P, :], pages[1][:])
